import numpy as np
import ml_dtypes


def mxq(x, axis, fmt="e4m3"):
    dtype, down = {"e4m3": (ml_dtypes.float8_e4m3fn, 7), "e5m2": (ml_dtypes.float8_e5m2, 14)}[fmt]
    v = np.moveaxis(np.asarray(x, np.float32).astype(ml_dtypes.bfloat16).astype(np.float64), axis, -1)
    blocks = v.reshape(v.shape[:-1] + (-1, 32))
    amax = np.abs(blocks).max(-1, keepdims=True)
    byte = np.maximum(np.where(amax > 0, np.frexp(amax)[1] - 1 + 127, 0) - down, 1)
    scale = np.exp2(byte - 127.0)
    codes = (blocks / scale).astype(np.float32).astype(dtype).astype(np.float64)
    return np.moveaxis((codes * scale).reshape(v.shape), -1, axis)


WIDE = False


def mx_kscale(k):
    if not WIDE:
        return np.ones(k)
    levels = np.array([10, -10, 5, -5, 0])
    if k % 512:
        return np.exp2(np.random.permutation(np.resize(levels, k // 32))).repeat(32)
    a = np.empty((k // 512, 16))
    for p in range(k // 512):
        a[p, :8] = np.random.permutation(np.resize(levels, 8))
        for g in range(8):
            far = levels[np.abs(levels - a[p, g]) >= 10]
            a[p, g + 8] = far[np.random.randint(len(far))]
    return np.exp2(a.ravel()).repeat(32)


def f64(x):
    return np.asarray(x).astype(np.float64)


def striped(idx):
    return np.tile(idx.reshape(-1, 16).T, (8, 1)).astype(np.uint16)


def unstriped(offs):
    return offs[:16].T.reshape(-1).astype(np.int64)


def silu(v):
    return v / (1.0 + np.exp(-np.maximum(v, -700.0)))


K, T, E, C, H, N = 1024, 1024, 4, 128, 512, 256


def by_expert(wq, xq):
    return np.concatenate([wq[e].T @ xq[:, e * C:(e + 1) * C] for e in range(E)], axis=1)


def setup_inputs():
    n = np.random.standard_normal
    s = mx_kscale(K)[:, None]
    u = mx_kscale(H)
    return {
        "xT": (n((K, T)) * s).astype(np.float32),
        "w1": (n((E, K, H)) / np.sqrt(K) / s[None] * u[None, None, :]).astype(np.float32),
        "w2": (n((E, H, N)) / np.sqrt(H) / u[None, :, None]).astype(np.float32),
        "gate": np.tile(np.random.uniform(0.2, 1.0, E * C), (N, 1)).astype(np.float32),
        "offs": striped(np.random.permutation(T)[:E * C]),
    }


def reference(xT, w1, w2, gate, offs):
    idx = unstriped(offs)
    xq = mxq(f64(xT)[:, idx], 0, "e4m3")
    h = silu(by_expert(mxq(f64(w1), 1, "e4m3"), xq))
    y = by_expert(mxq(f64(w2), 1, "e4m3"), mxq(h, 0, "e4m3"))
    out = np.zeros((N, T))
    out[:, idx] = f64(gate) * y
    return out

@@ -1,0 +1,225 @@
+from contextlib import ExitStack
+
+import concourse.mybir as mybir
+
+K, T, E, C, H, N = 1024, 1024, 4, 128, 512, 256
+S = E * C
+FLOPS = 2 * S * K * H + 2 * S * H * N
+
+F32 = mybir.dt.float32
+BF16 = mybir.dt.bfloat16
+U32 = mybir.dt.uint32
+U16 = mybir.dt.uint16
+U8 = mybir.dt.uint8
+FP8X4 = mybir.dt.float8_e4m3fn_x4
+SILU = mybir.ActivationFunctionType.Silu
+MULT = mybir.AluOpType.mult
+ADD = mybir.AluOpType.add
+
+P = 128
+G = K // 512
+NB = N // P
+
+X_SHARES = (160, 96, 0)
+W1_SHARES = (64, 0, 64)
+W1_SHARES_LAST = (40, 0, 88)
+W2_SHARES = (64, 0, 0)
+
+
+def tile_routed_moe_kernel(tc, xT, w1, w2, gate, offs, out):
+    nc = tc.nc
+    with ExitStack() as ctx:
+        lists = ctx.enter_context(tc.tile_pool(name="lists", bufs=1))
+        raw = ctx.enter_context(tc.tile_pool(name="raw", bufs=1))
+        keep = ctx.enter_context(tc.tile_pool(name="keep", bufs=1))
+        psum = ctx.enter_context(tc.psum_pool(name="psum", bufs=4))
+
+        def shared_copy(dst, src, shares):
+            a, b, c = shares
+            if c:
+                nc.vector.tensor_copy(out=dst[:, a + b :], in_=src[:, a + b :])
+            if a:
+                nc.scalar.copy(out=dst[:, :a], in_=src[:, :a])
+            if b:
+                nc.gpsimd.tensor_scalar(
+                    out=dst[:, a : a + b], in0=src[:, a : a + b], scalar1=1.0, scalar2=0.0, op0=MULT, op1=ADD
+                )
+
+        offs_sb = lists.tile([P, S // 16], U16, name="offs_sb")
+        nc.sync.dma_start(offs_sb[:], offs)
+
+        x_view = xT.rearrange("(g p u e) n -> g u p e n", g=G, p=P, u=2, e=2)
+        x_raw = {}
+        for g in range(G):
+            for u in range(2):
+                x_raw[g, u] = raw.tile([P, 2, T], F32, name="x_raw%d%d" % (g, u))
+                nc.sync.dma_start(x_raw[g, u][:], x_view[g, u])
+
+        w1_raw = {}
+        w2_raw = {}
+        gate_sb = raw.tile([P, NB, S], F32, name="gate_sb")
+
+        def load_w1(e, g):
+            w1_raw[e, g] = raw.tile([P, 4, H], F32, name="w1_raw%d%d" % (e, g), tag="w1_raw%d%d" % (e, g), align_bytes=64)
+            nc.sync.dma_start(
+                w1_raw[e, g][:],
+                w1[e, g * 512 : (g + 1) * 512, :].rearrange("(p j) c -> p j c", j=4),
+            )
+
+        def load_w2(e):
+            w2_raw[e] = raw.tile([P, 4, N], F32, name="w2_raw%d" % e)
+            nc.sync.dma_start(w2_raw[e][:], w2[e].rearrange("(p j) n -> p j n", j=4))
+
+        for e in range(E):
+            for g in range(G):
+                load_w1(e, g)
+            load_w2(e)
+            if e == 0:
+                nc.sync.dma_start(gate_sb[:], gate.rearrange("(b p) s -> p b s", p=P))
+
+        zero = keep.tile([P, 1], F32, name="zero")
+        warm = keep.tile([P, 1], F32, name="warm")
+        nc.vector.memset(zero[:], 0.0)
+        nc.scalar.activation(out=warm[:], in_=zero[:], func=SILU)
+        win = []
+        for b in range(NB):
+            win.append(keep.tile([P, T], F32, name="win%d" % b))
+            nc.vector.memset(win[b][:], 0.0)
+
+        x_codes = []
+        x_scales = []
+        for g in range(G):
+            x_grouped = keep.tile([P, S * 4], BF16, name="x_grouped%d" % g, align_bytes=64)
+            grouped_words = x_grouped[:].bitcast(U32).rearrange("p (s u) -> p s u", u=2)
+            for u in range(2):
+                pairs = keep.tile([P, T * 2], BF16, name="pairs%d%d" % (g, u), align_bytes=64)
+                shared_copy(
+                    pairs[:].rearrange("p (c i e) -> p c e i", i=4, e=2),
+                    x_raw[g, u][:].rearrange("p e (c i) -> p c e i", i=4),
+                    X_SHARES,
+                )
+                nc.vector.tensor_copy(
+                    out=grouped_words[:, :, u],
+                    in_=pairs[:].bitcast(U32).indirect(offs_sb[:]),
+                )
+            x_codes.append(keep.tile([P, S], U32, name="x_codes%d" % g, align_bytes=64))
+            x_scales.append(keep.tile([P, S], U8, name="x_scales%d" % g, align_bytes=64))
+            nc.vector.quantize_mx(out=x_codes[g][:].bitcast(FP8X4), scales=x_scales[g][:], in_=x_grouped[:])
+
+        t_ = {}
+
+        def w1_copy(e, g):
+            t_["w1g", e, g] = keep.tile(
+                [P, 4 * H], BF16, name="w1_grouped%d%d" % (e, g), tag="w1_grouped%d%d" % (e, g), align_bytes=64
+            )
+            shared_copy(
+                t_["w1g", e, g][:].rearrange("p (t m j) -> p m j t", t=4, j=4),
+                w1_raw[e, g][:].rearrange("p j (m t) -> p m j t", t=4),
+                W1_SHARES_LAST if (e == E - 1 and g == G - 1) else W1_SHARES,
+            )
+
+        def w1_quant(e, g):
+            t_["w1c", e, g] = keep.tile([P, H], U32, name="w1_codes%d%d" % (e, g), align_bytes=64)
+            t_["w1s", e, g] = keep.tile([P, H], U8, name="w1_scales%d%d" % (e, g), align_bytes=64)
+            nc.vector.quantize_mx(
+                out=t_["w1c", e, g][:].bitcast(FP8X4), scales=t_["w1s", e, g][:], in_=t_["w1g", e, g][:]
+            )
+
+        def w2_copy(e):
+            t_["w2g", e] = keep.tile([P, 4 * N], BF16, name="w2_grouped%d" % e, align_bytes=64)
+            shared_copy(
+                t_["w2g", e][:].rearrange("p (c i j) -> p c j i", i=4, j=4),
+                w2_raw[e][:].rearrange("p j (c i) -> p c j i", i=4),
+                W2_SHARES,
+            )
+
+        def w2_quant(e):
+            t_["w2c", e] = keep.tile([P, N], U32, name="w2_codes%d" % e, align_bytes=64)
+            t_["w2s", e] = keep.tile([P, N], U8, name="w2_scales%d" % e, align_bytes=64)
+            nc.vector.quantize_mx(out=t_["w2c", e][:].bitcast(FP8X4), scales=t_["w2s", e][:], in_=t_["w2g", e][:])
+
+        def layer1(e):
+            slots = slice(e * C, (e + 1) * C)
+            acc1 = psum.tile([P, 4, C], F32)
+            t_["acc1", e] = acc1
+            for t in range(4):
+                cols = slice(t * P, (t + 1) * P)
+                for g in range(G):
+                    nc.tensor.matmul_mx(
+                        out=acc1[:, t, :],
+                        lhsT=t_["w1c", e, g][:, cols].bitcast(FP8X4),
+                        lhsT_scale=t_["w1s", e, g][:, cols],
+                        rhs=x_codes[g][:, slots].bitcast(FP8X4),
+                        rhs_scale=x_scales[g][:, slots],
+                        start=(g == 0),
+                        stop=(g == G - 1),
+                    )
+
+        def silu(e):
+            t_["hg", e] = raw.tile([P, C * 4], BF16, name="h_grouped%d" % e, tag="w1_raw%d0" % (e + 1), align_bytes=64)
+            nc.scalar.activation(
+                out=t_["hg", e][:].rearrange("p (c t) -> p c t", t=4),
+                in_=t_["acc1", e][:].rearrange("p t c -> p c t"),
+                func=SILU,
+            )
+
+        def h_quant(e):
+            t_["hc", e] = keep.tile([P, C], U32, name="h_codes%d" % e, tag="w1_grouped%d0" % (e + 1), align_bytes=64)
+            t_["hs", e] = keep.tile([P, C], U8, name="h_scales%d" % e, align_bytes=64)
+            nc.vector.quantize_mx(out=t_["hc", e][:].bitcast(FP8X4), scales=t_["hs", e][:], in_=t_["hg", e][:])
+
+        def layer2(e):
+            acc2 = psum.tile([P, NB, C], F32)
+            t_["acc2", e] = acc2
+            for b in range(NB):
+                cols = slice(b * P, (b + 1) * P)
+                nc.tensor.matmul_mx(
+                    out=acc2[:, b, :],
+                    lhsT=t_["w2c", e][:, cols].bitcast(FP8X4),
+                    lhsT_scale=t_["w2s", e][:, cols],
+                    rhs=t_["hc", e][:].bitcast(FP8X4),
+                    rhs_scale=t_["hs", e][:],
+                    start=True,
+                    stop=True,
+                )
+
+        def gated(e):
+            t_["y", e] = keep.tile([P, NB, C], F32, name="y_sb%d" % e, tag="w1_grouped%d1" % (e + 1), align_bytes=64)
+            nc.vector.tensor_tensor(
+                out=t_["y", e][:], in0=t_["acc2", e][:], in1=gate_sb[:, :, e * C : (e + 1) * C], op=MULT
+            )
+
+        def scatter(e, b):
+            nc.vector.tensor_copy(
+                out=win[b][:].indirect(offs_sb[:, e * (C // 16) : (e + 1) * (C // 16)]),
+                in_=t_["y", e][:, b, :],
+            )
+
+        for e in range(E):
+            p = e - 1
+            w1_copy(e, 0)
+            if p >= 0:
+                silu(p)
+            w1_quant(e, 0)
+            w1_copy(e, 1)
+            if p >= 0:
+                h_quant(p)
+                layer2(p)
+            w2_copy(e)
+            w1_quant(e, 1)
+            layer1(e)
+            if p >= 0:
+                gated(p)
+                scatter(p, 0)
+            w2_quant(e)
+            if p >= 0:
+                scatter(p, 1)
+        silu(E - 1)
+        h_quant(E - 1)
+        layer2(E - 1)
+        gated(E - 1)
+        scatter(E - 1, 0)
+        scatter(E - 1, 1)
+
+        for b in range(NB):
+            nc.sync.dma_start(out[b * P : (b + 1) * P, :], win[b][:])

@@ -185,14 +185,14 @@ def tile_routed_moe_kernel(tc, xT, w1, w2, gate, offs, out):
 
         def gated(e):
             t_["y", e] = keep.tile([P, NB, C], F32, name="y_sb%d" % e, tag="w1_grouped%d1" % (e + 1), align_bytes=64)
-            nc.vector.tensor_tensor(
-                out=t_["y", e][:], in0=t_["acc2", e][:], in1=gate_sb[:, :, e * C : (e + 1) * C], op=MULT
-            )
+            nc.scalar.copy(out=t_["y", e][:], in_=t_["acc2", e][:])
 
         def scatter(e, b):
-            nc.vector.tensor_copy(
+            nc.vector.tensor_tensor(
                 out=win[b][:].indirect(offs_sb[:, e * (C // 16) : (e + 1) * (C // 16)]),
-                in_=t_["y", e][:, b, :],
+                in0=t_["y", e][:, b, :],
+                in1=gate_sb[:, b, e * C : (e + 1) * C],
+                op=MULT,
             )
 
         for e in range(E):

@@ -57,7 +57,8 @@ def tile_routed_moe_kernel(tc, xT, w1, w2, gate, offs, out):
 
         w1_raw = {}
         w2_raw = {}
-        gate_sb = raw.tile([P, NB, S], F32, name="gate_sb")
+        gate_view = gate.rearrange("(b p) (h s) -> h p b s", p=P, h=2)
+        gate_sb = [raw.tile([P, NB, S // 2], F32, name="gate_sb%d" % h) for h in range(2)]
 
         def load_w1(e, g):
             w1_raw[e, g] = raw.tile([P, 4, H], F32, name="w1_raw%d%d" % (e, g), tag="w1_raw%d%d" % (e, g), align_bytes=64)
@@ -75,7 +76,8 @@ def tile_routed_moe_kernel(tc, xT, w1, w2, gate, offs, out):
                 load_w1(e, g)
             load_w2(e)
             if e == 0:
-                nc.sync.dma_start(gate_sb[:], gate.rearrange("(b p) s -> p b s", p=P))
+                nc.sync.dma_start(gate_sb[0][:], gate_view[0])
+        nc.sync.dma_start(gate_sb[1][:], gate_view[1])
 
         zero = keep.tile([P, 1], F32, name="zero")
         warm = keep.tile([P, 1], F32, name="warm")
@@ -191,7 +193,7 @@ def tile_routed_moe_kernel(tc, xT, w1, w2, gate, offs, out):
             nc.vector.tensor_tensor(
                 out=win[b][:].indirect(offs_sb[:, e * (C // 16) : (e + 1) * (C // 16)]),
                 in0=t_["y", e][:, b, :],
-                in1=gate_sb[:, b, e * C : (e + 1) * C],
+                in1=gate_sb[e // 2][:, b, (e % 2) * C : (e % 2 + 1) * C],
                 op=MULT,
             )
 

@@ -21,7 +21,7 @@ G = K // 512
 NB = N // P
 
 X_SHARES = (160, 96, 0)
-W1_SHARES = (64, 0, 64)
+W1_SHARES = ((96, 0, 32), (32, 0, 96))
 W1_SHARES_LAST = (40, 0, 88)
 W2_SHARES = (64, 0, 0)
 
@@ -75,7 +75,7 @@ def tile_routed_moe_kernel(tc, xT, w1, w2, gate, offs, out):
             for g in range(G):
                 load_w1(e, g)
             load_w2(e)
-            if e == 0:
+            if e == 1:
                 nc.sync.dma_start(gate_sb[0][:], gate_view[0])
         nc.sync.dma_start(gate_sb[1][:], gate_view[1])
 
@@ -117,7 +117,7 @@ def tile_routed_moe_kernel(tc, xT, w1, w2, gate, offs, out):
             shared_copy(
                 t_["w1g", e, g][:].rearrange("p (t m j) -> p m j t", t=4, j=4),
                 w1_raw[e, g][:].rearrange("p j (m t) -> p m j t", t=4),
-                W1_SHARES_LAST if (e == E - 1 and g == G - 1) else W1_SHARES,
+                W1_SHARES_LAST if (e == E - 1 and g == G - 1) else W1_SHARES[g],
             )
 
         def w1_quant(e, g):

@@ -22,7 +22,7 @@ NB = N // P
 
 X_SHARES = (160, 96, 0)
 W1_SHARES = ((96, 0, 32), (32, 0, 96))
-W1_SHARES_LAST = (40, 0, 88)
+W1_SHARES_LAST = (20, 0, 44)
 W2_SHARES = (64, 0, 0)
 
 
@@ -61,11 +61,16 @@ def tile_routed_moe_kernel(tc, xT, w1, w2, gate, offs, out):
         gate_sb = [raw.tile([P, NB, S // 2], F32, name="gate_sb%d" % h) for h in range(2)]
 
         def load_w1(e, g):
+            rows = w1[e, g * 512 : (g + 1) * 512, :].rearrange("(p j) c -> p j c", j=4)
+            if e == E - 1 and g == G - 1:
+                w1_raw[e, g] = []
+                for half in range(2):
+                    piece = raw.tile([P, 4, H // 2], F32, name="w1_raw%d%d%d" % (e, g, half), align_bytes=64)
+                    nc.sync.dma_start(piece[:], rows[:, :, half * (H // 2) : (half + 1) * (H // 2)])
+                    w1_raw[e, g].append(piece)
+                return
             w1_raw[e, g] = raw.tile([P, 4, H], F32, name="w1_raw%d%d" % (e, g), tag="w1_raw%d%d" % (e, g), align_bytes=64)
-            nc.sync.dma_start(
-                w1_raw[e, g][:],
-                w1[e, g * 512 : (g + 1) * 512, :].rearrange("(p j) c -> p j c", j=4),
-            )
+            nc.sync.dma_start(w1_raw[e, g][:], rows)
 
         def load_w2(e):
             w2_raw[e] = raw.tile([P, 4, N], F32, name="w2_raw%d" % e)
@@ -114,18 +119,32 @@ def tile_routed_moe_kernel(tc, xT, w1, w2, gate, offs, out):
             t_["w1g", e, g] = keep.tile(
                 [P, 4 * H], BF16, name="w1_grouped%d%d" % (e, g), tag="w1_grouped%d%d" % (e, g), align_bytes=64
             )
-            shared_copy(
-                t_["w1g", e, g][:].rearrange("p (t m j) -> p m j t", t=4, j=4),
-                w1_raw[e, g][:].rearrange("p j (m t) -> p m j t", t=4),
-                W1_SHARES_LAST if (e == E - 1 and g == G - 1) else W1_SHARES[g],
-            )
+            grouped = t_["w1g", e, g][:].rearrange("p (t m j) -> p m j t", t=4, j=4)
+            if e == E - 1 and g == G - 1:
+                for half in range(2):
+                    shared_copy(
+                        grouped[:, half * (P // 2) : (half + 1) * (P // 2)],
+                        w1_raw[e, g][half][:].rearrange("p j (m t) -> p m j t", t=4),
+                        W1_SHARES_LAST,
+                    )
+                return
+            shared_copy(grouped, w1_raw[e, g][:].rearrange("p j (m t) -> p m j t", t=4), W1_SHARES[g])
 
         def w1_quant(e, g):
-            t_["w1c", e, g] = keep.tile([P, H], U32, name="w1_codes%d%d" % (e, g), align_bytes=64)
-            t_["w1s", e, g] = keep.tile([P, H], U8, name="w1_scales%d%d" % (e, g), align_bytes=64)
-            nc.vector.quantize_mx(
-                out=t_["w1c", e, g][:].bitcast(FP8X4), scales=t_["w1s", e, g][:], in_=t_["w1g", e, g][:]
-            )
+            pieces = 2 if (e == E - 1 and g == G - 1) else 1
+            width = H // pieces
+            t_["w1c", e, g] = []
+            t_["w1s", e, g] = []
+            for h in range(pieces):
+                codes = keep.tile([P, width], U32, name="w1_codes%d%d%d" % (e, g, h), align_bytes=64)
+                scales = keep.tile([P, width], U8, name="w1_scales%d%d%d" % (e, g, h), align_bytes=64)
+                nc.vector.quantize_mx(
+                    out=codes[:].bitcast(FP8X4),
+                    scales=scales[:],
+                    in_=t_["w1g", e, g][:, 4 * h * width : 4 * (h + 1) * width],
+                )
+                t_["w1c", e, g].append(codes)
+                t_["w1s", e, g].append(scales)
 
         def w2_copy(e):
             t_["w2g", e] = keep.tile([P, 4 * N], BF16, name="w2_grouped%d" % e, align_bytes=64)
@@ -142,15 +161,17 @@ def tile_routed_moe_kernel(tc, xT, w1, w2, gate, offs, out):
 
         def layer1(e):
             slots = slice(e * C, (e + 1) * C)
-            acc1 = psum.tile([P, 4, C], F32)
+            acc1 = psum.tile([P, 4, C], F32, bufs=3)
             t_["acc1", e] = acc1
             for t in range(4):
-                cols = slice(t * P, (t + 1) * P)
                 for g in range(G):
+                    tiles_each = 4 // len(t_["w1c", e, g])
+                    h = t // tiles_each
+                    cols = slice((t % tiles_each) * P, (t % tiles_each + 1) * P)
                     nc.tensor.matmul_mx(
                         out=acc1[:, t, :],
-                        lhsT=t_["w1c", e, g][:, cols].bitcast(FP8X4),
-                        lhsT_scale=t_["w1s", e, g][:, cols],
+                        lhsT=t_["w1c", e, g][h][:, cols].bitcast(FP8X4),
+                        lhsT_scale=t_["w1s", e, g][h][:, cols],
                         rhs=x_codes[g][:, slots].bitcast(FP8X4),
                         rhs_scale=x_scales[g][:, slots],
                         start=(g == 0),
@@ -171,12 +192,16 @@ def tile_routed_moe_kernel(tc, xT, w1, w2, gate, offs, out):
             nc.vector.quantize_mx(out=t_["hc", e][:].bitcast(FP8X4), scales=t_["hs", e][:], in_=t_["hg", e][:])
 
         def layer2(e):
-            acc2 = psum.tile([P, NB, C], F32)
-            t_["acc2", e] = acc2
+            if e == E - 1:
+                banks = [psum.tile([P, C], F32, name="acc2_last%d" % b, bufs=1) for b in range(NB)]
+                t_["acc2b", e] = banks
+            else:
+                acc2 = psum.tile([P, NB, C], F32, bufs=3)
+                t_["acc2", e] = acc2
             for b in range(NB):
                 cols = slice(b * P, (b + 1) * P)
                 nc.tensor.matmul_mx(
-                    out=acc2[:, b, :],
+                    out=banks[b][:] if e == E - 1 else acc2[:, b, :],
                     lhsT=t_["w2c", e][:, cols].bitcast(FP8X4),
                     lhsT_scale=t_["w2s", e][:, cols],
                     rhs=t_["hc", e][:].bitcast(FP8X4),
@@ -187,12 +212,23 @@ def tile_routed_moe_kernel(tc, xT, w1, w2, gate, offs, out):
 
         def gated(e):
             t_["y", e] = keep.tile([P, NB, C], F32, name="y_sb%d" % e, tag="w1_grouped%d1" % (e + 1), align_bytes=64)
-            nc.scalar.copy(out=t_["y", e][:], in_=t_["acc2", e][:])
+            if e == E - 1:
+                for b in range(NB):
+                    nc.scalar.copy(out=t_["y", e][:, b, :], in_=t_["acc2b", e][b][:])
+            else:
+                nc.scalar.copy(out=t_["y", e][:], in_=t_["acc2", e][:])
+
+        def gated_block(e, b):
+            if b == 0:
+                t_["yb", e, b] = keep.tile([P, C], F32, name="y_sb%d%d" % (e, b), tag="w1_grouped%d1" % (e + 1), align_bytes=64)
+            else:
+                t_["yb", e, b] = keep.tile([P, C], F32, name="y_sb%d%d" % (e, b), tag="w2_grouped%d" % (e + 1), align_bytes=64)
+            nc.scalar.copy(out=t_["yb", e, b][:], in_=t_["acc2", e][:, b, :])
 
         def scatter(e, b):
             nc.vector.tensor_tensor(
                 out=win[b][:].indirect(offs_sb[:, e * (C // 16) : (e + 1) * (C // 16)]),
-                in0=t_["y", e][:, b, :],
+                in0=t_["yb", e, b][:] if ("yb", e, b) in t_ else t_["y", e][:, b, :],
                 in1=gate_sb[e // 2][:, b, (e % 2) * C : (e % 2 + 1) * C],
                 op=MULT,
             )
@@ -210,12 +246,17 @@ def tile_routed_moe_kernel(tc, xT, w1, w2, gate, offs, out):
             w2_copy(e)
             w1_quant(e, 1)
             layer1(e)
-            if p >= 0:
+            if 0 <= p < E - 2:
                 gated(p)
                 scatter(p, 0)
+            if p == E - 2:
+                gated_block(p, 0)
+                scatter(p, 0)
             w2_quant(e)
-            if p >= 0:
+            if 0 <= p < E - 2:
                 scatter(p, 1)
+        gated_block(E - 2, 1)
+        scatter(E - 2, 1)
         silu(E - 1)
         h_quant(E - 1)
         layer2(E - 1)

@@ -20,7 +20,7 @@ P = 128
 G = K // 512
 NB = N // P
 
-X_SHARES = (160, 96, 0)
+X_SHARES = (128, 128, 0)
 W1_SHARES = ((96, 0, 32), (32, 0, 96))
 W1_SHARES_LAST = (20, 0, 44)
 W2_SHARES = (64, 0, 0)

@@ -46,7 +46,6 @@ def tile_routed_moe_kernel(tc, xT, w1, w2, gate, offs, out):
                 )
 
         offs_sb = lists.tile([P, S // 16], U16, name="offs_sb")
-        nc.sync.dma_start(offs_sb[:], offs)
 
         x_view = xT.rearrange("(g p u e) n -> g u p e n", g=G, p=P, u=2, e=2)
         x_raw = {}
@@ -54,6 +53,8 @@ def tile_routed_moe_kernel(tc, xT, w1, w2, gate, offs, out):
             for u in range(2):
                 x_raw[g, u] = raw.tile([P, 2, T], F32, name="x_raw%d%d" % (g, u))
                 nc.sync.dma_start(x_raw[g, u][:], x_view[g, u])
+                if g == 0 and u == 0:
+                    nc.sync.dma_start(offs_sb[:], offs)
 
         w1_raw = {}
         w2_raw = {}

@@ -98,7 +98,7 @@ def tile_routed_moe_kernel(tc, xT, w1, w2, gate, offs, out):
         x_scales = []
         for g in range(G):
             x_grouped = keep.tile([P, S * 4], BF16, name="x_grouped%d" % g, align_bytes=64)
-            grouped_words = x_grouped[:].bitcast(U32).rearrange("p (s u) -> p s u", u=2)
+            gathered = keep.tile([P, 2 * S * 2], BF16, name="gathered%d" % g, align_bytes=64)
             for u in range(2):
                 pairs = keep.tile([P, T * 2], BF16, name="pairs%d%d" % (g, u), align_bytes=64)
                 shared_copy(
@@ -107,9 +107,13 @@ def tile_routed_moe_kernel(tc, xT, w1, w2, gate, offs, out):
                     X_SHARES,
                 )
                 nc.vector.tensor_copy(
-                    out=grouped_words[:, :, u],
+                    out=gathered[:, u * S * 2 : (u + 1) * S * 2].bitcast(U32),
                     in_=pairs[:].bitcast(U32).indirect(offs_sb[:]),
                 )
+            nc.vector.tensor_copy(
+                out=x_grouped[:].rearrange("p (s u e) -> p s u e", u=2, e=2),
+                in_=gathered[:].rearrange("p (u s e) -> p s u e", u=2, e=2),
+            )
             x_codes.append(keep.tile([P, S], U32, name="x_codes%d" % g, align_bytes=64))
             x_scales.append(keep.tile([P, S], U8, name="x_scales%d" % g, align_bytes=64))
             nc.vector.quantize_mx(out=x_codes[g][:].bitcast(FP8X4), scales=x_scales[g][:], in_=x_grouped[:])

@@ -20,7 +20,7 @@ P = 128
 G = K // 512
 NB = N // P
 
-X_SHARES = (128, 128, 0)
+X_SHARES = (144, 112, 0)
 W1_SHARES = ((96, 0, 32), (32, 0, 96))
 W1_SHARES_LAST = (20, 0, 44)
 W2_SHARES = (64, 0, 0)
@@ -47,14 +47,15 @@ def tile_routed_moe_kernel(tc, xT, w1, w2, gate, offs, out):
 
         offs_sb = lists.tile([P, S // 16], U16, name="offs_sb")
 
-        x_view = xT.rearrange("(g p u e) n -> g u p e n", g=G, p=P, u=2, e=2)
+        x_view = xT.rearrange("(g p f) n -> g p f n", g=G, p=P, f=4)
         x_raw = {}
         for g in range(G):
+            x_pass = raw.tile([P, 4, T], F32, name="x_pass%d" % g)
+            nc.sync.dma_start(x_pass[:], x_view[g])
             for u in range(2):
-                x_raw[g, u] = raw.tile([P, 2, T], F32, name="x_raw%d%d" % (g, u))
-                nc.sync.dma_start(x_raw[g, u][:], x_view[g, u])
-                if g == 0 and u == 0:
-                    nc.sync.dma_start(offs_sb[:], offs)
+                x_raw[g, u] = x_pass[:, 2 * u : 2 * u + 2, :]
+            if g == 0:
+                nc.sync.dma_start(offs_sb[:], offs)
 
         w1_raw = {}
         w2_raw = {}
@@ -77,9 +78,14 @@ def tile_routed_moe_kernel(tc, xT, w1, w2, gate, offs, out):
             w2_raw[e] = raw.tile([P, 4, N], F32, name="w2_raw%d" % e)
             nc.sync.dma_start(w2_raw[e][:], w2[e].rearrange("(p j) n -> p j n", j=4))
 
+        w1_first = raw.tile([P, G, 4, H], F32, name="w1_first", align_bytes=64)
+        nc.sync.dma_start(w1_first[:], w1[0].rearrange("(g p j) c -> p g j c", g=G, j=4))
+        for g in range(G):
+            w1_raw[0, g] = w1_first[:, g]
         for e in range(E):
             for g in range(G):
-                load_w1(e, g)
+                if e > 0:
+                    load_w1(e, g)
             load_w2(e)
             if e == 1:
                 nc.sync.dma_start(gate_sb[0][:], gate_view[0])
@@ -103,7 +109,7 @@ def tile_routed_moe_kernel(tc, xT, w1, w2, gate, offs, out):
                 pairs = keep.tile([P, T * 2], BF16, name="pairs%d%d" % (g, u), align_bytes=64)
                 shared_copy(
                     pairs[:].rearrange("p (c i e) -> p c e i", i=4, e=2),
-                    x_raw[g, u][:].rearrange("p e (c i) -> p c e i", i=4),
+                    x_raw[g, u].rearrange("p e (c i) -> p c e i", i=4),
                     X_SHARES,
                 )
                 nc.vector.tensor_copy(
@@ -133,7 +139,7 @@ def tile_routed_moe_kernel(tc, xT, w1, w2, gate, offs, out):
                         W1_SHARES_LAST,
                     )
                 return
-            shared_copy(grouped, w1_raw[e, g][:].rearrange("p j (m t) -> p m j t", t=4), W1_SHARES[g])
+            shared_copy(grouped, (w1_raw[e, g] if e == 0 else w1_raw[e, g][:]).rearrange("p j (m t) -> p m j t", t=4), W1_SHARES[g])
 
         def w1_quant(e, g):
             pieces = 2 if (e == E - 1 and g == G - 1) else 1

@@ -21,7 +21,7 @@ G = K // 512
 NB = N // P
 
 X_SHARES = (144, 112, 0)
-W1_SHARES = ((96, 0, 32), (32, 0, 96))
+W1_SHARES = ((96, 0, 32), (48, 0, 80))
 W1_SHARES_LAST = (20, 0, 44)
 W2_SHARES = (64, 0, 0)
 
@@ -142,20 +142,21 @@ def tile_routed_moe_kernel(tc, xT, w1, w2, gate, offs, out):
             shared_copy(grouped, (w1_raw[e, g] if e == 0 else w1_raw[e, g][:]).rearrange("p j (m t) -> p m j t", t=4), W1_SHARES[g])
 
         def w1_quant(e, g):
-            pieces = 2 if (e == E - 1 and g == G - 1) else 1
-            width = H // pieces
+            pieces = (1, 1, 2) if (e == E - 1 and g == G - 1) else (4,)
             t_["w1c", e, g] = []
-            t_["w1s", e, g] = []
-            for h in range(pieces):
+            t = 0
+            for h, tiles in enumerate(pieces):
+                width = tiles * P
                 codes = keep.tile([P, width], U32, name="w1_codes%d%d%d" % (e, g, h), align_bytes=64)
                 scales = keep.tile([P, width], U8, name="w1_scales%d%d%d" % (e, g, h), align_bytes=64)
                 nc.vector.quantize_mx(
                     out=codes[:].bitcast(FP8X4),
                     scales=scales[:],
-                    in_=t_["w1g", e, g][:, 4 * h * width : 4 * (h + 1) * width],
+                    in_=t_["w1g", e, g][:, 4 * P * t : 4 * P * (t + tiles)],
                 )
-                t_["w1c", e, g].append(codes)
-                t_["w1s", e, g].append(scales)
+                for i in range(tiles):
+                    t_["w1c", e, g].append((codes[:, i * P : (i + 1) * P], scales[:, i * P : (i + 1) * P]))
+                t += tiles
 
         def w2_copy(e):
             t_["w2g", e] = keep.tile([P, 4 * N], BF16, name="w2_grouped%d" % e, align_bytes=64)
@@ -176,13 +177,11 @@ def tile_routed_moe_kernel(tc, xT, w1, w2, gate, offs, out):
             t_["acc1", e] = acc1
             for t in range(4):
                 for g in range(G):
-                    tiles_each = 4 // len(t_["w1c", e, g])
-                    h = t // tiles_each
-                    cols = slice((t % tiles_each) * P, (t % tiles_each + 1) * P)
+                    codes, scales = t_["w1c", e, g][t]
                     nc.tensor.matmul_mx(
                         out=acc1[:, t, :],
-                        lhsT=t_["w1c", e, g][h][:, cols].bitcast(FP8X4),
-                        lhsT_scale=t_["w1s", e, g][h][:, cols],
+                        lhsT=codes.bitcast(FP8X4),
+                        lhsT_scale=scales,
                         rhs=x_codes[g][:, slots].bitcast(FP8X4),
                         rhs_scale=x_scales[g][:, slots],
                         start=(g == 0),

from contextlib import ExitStack

import concourse.mybir as mybir

K, T, E, C, H, N = 1024, 1024, 4, 128, 512, 256
S = E * C
FLOPS = 2 * S * K * H + 2 * S * H * N

F32 = mybir.dt.float32
BF16 = mybir.dt.bfloat16
U32 = mybir.dt.uint32
U16 = mybir.dt.uint16
U8 = mybir.dt.uint8
FP8X4 = mybir.dt.float8_e4m3fn_x4
SILU = mybir.ActivationFunctionType.Silu
MULT = mybir.AluOpType.mult
ADD = mybir.AluOpType.add

P = 128
G = K // 512
NB = N // P

X_SHARES = (144, 112, 0)
W1_SHARES = ((96, 0, 32), (48, 0, 80))
W1_SHARES_LAST = (20, 0, 44)
W2_SHARES = (64, 0, 0)


def tile_routed_moe_kernel(tc, xT, w1, w2, gate, offs, out):
    nc = tc.nc
    with ExitStack() as ctx:
        lists = ctx.enter_context(tc.tile_pool(name="lists", bufs=1))
        raw = ctx.enter_context(tc.tile_pool(name="raw", bufs=1))
        keep = ctx.enter_context(tc.tile_pool(name="keep", bufs=1))
        psum = ctx.enter_context(tc.psum_pool(name="psum", bufs=4))

        def shared_copy(dst, src, shares):
            a, b, c = shares
            if c:
                nc.vector.tensor_copy(out=dst[:, a + b :], in_=src[:, a + b :])
            if a:
                nc.scalar.copy(out=dst[:, :a], in_=src[:, :a])
            if b:
                nc.gpsimd.tensor_scalar(
                    out=dst[:, a : a + b], in0=src[:, a : a + b], scalar1=1.0, scalar2=0.0, op0=MULT, op1=ADD
                )

        offs_sb = lists.tile([P, S // 16], U16, name="offs_sb")

        x_view = xT.rearrange("(g p f) n -> g p f n", g=G, p=P, f=4)
        x_raw = {}
        for g in range(G):
            x_pass = raw.tile([P, 4, T], F32, name="x_pass%d" % g)
            nc.sync.dma_start(x_pass[:], x_view[g])
            for u in range(2):
                x_raw[g, u] = x_pass[:, 2 * u : 2 * u + 2, :]
            if g == 0:
                nc.sync.dma_start(offs_sb[:], offs)

        w1_raw = {}
        w2_raw = {}
        gate_view = gate.rearrange("(b p) (h s) -> h p b s", p=P, h=2)
        gate_sb = [raw.tile([P, NB, S // 2], F32, name="gate_sb%d" % h) for h in range(2)]

        def load_w1(e, g):
            rows = w1[e, g * 512 : (g + 1) * 512, :].rearrange("(p j) c -> p j c", j=4)
            if e == E - 1 and g == G - 1:
                w1_raw[e, g] = []
                for half in range(2):
                    piece = raw.tile([P, 4, H // 2], F32, name="w1_raw%d%d%d" % (e, g, half), align_bytes=64)
                    nc.sync.dma_start(piece[:], rows[:, :, half * (H // 2) : (half + 1) * (H // 2)])
                    w1_raw[e, g].append(piece)
                return
            w1_raw[e, g] = raw.tile([P, 4, H], F32, name="w1_raw%d%d" % (e, g), tag="w1_raw%d%d" % (e, g), align_bytes=64)
            nc.sync.dma_start(w1_raw[e, g][:], rows)

        def load_w2(e):
            w2_raw[e] = raw.tile([P, 4, N], F32, name="w2_raw%d" % e)
            nc.sync.dma_start(w2_raw[e][:], w2[e].rearrange("(p j) n -> p j n", j=4))

        w1_first = raw.tile([P, G, 4, H], F32, name="w1_first", align_bytes=64)
        nc.sync.dma_start(w1_first[:], w1[0].rearrange("(g p j) c -> p g j c", g=G, j=4))
        for g in range(G):
            w1_raw[0, g] = w1_first[:, g]
        for e in range(E):
            for g in range(G):
                if e > 0:
                    load_w1(e, g)
            load_w2(e)
            if e == 1:
                nc.sync.dma_start(gate_sb[0][:], gate_view[0])
        nc.sync.dma_start(gate_sb[1][:], gate_view[1])

        zero = keep.tile([P, 1], F32, name="zero")
        warm = keep.tile([P, 1], F32, name="warm")
        nc.vector.memset(zero[:], 0.0)
        nc.scalar.activation(out=warm[:], in_=zero[:], func=SILU)
        win = []
        for b in range(NB):
            win.append(keep.tile([P, T], F32, name="win%d" % b))
            nc.vector.memset(win[b][:], 0.0)

        x_codes = []
        x_scales = []
        for g in range(G):
            x_grouped = keep.tile([P, S * 4], BF16, name="x_grouped%d" % g, align_bytes=64)
            gathered = keep.tile([P, 2 * S * 2], BF16, name="gathered%d" % g, align_bytes=64)
            for u in range(2):
                pairs = keep.tile([P, T * 2], BF16, name="pairs%d%d" % (g, u), align_bytes=64)
                shared_copy(
                    pairs[:].rearrange("p (c i e) -> p c e i", i=4, e=2),
                    x_raw[g, u].rearrange("p e (c i) -> p c e i", i=4),
                    X_SHARES,
                )
                nc.vector.tensor_copy(
                    out=gathered[:, u * S * 2 : (u + 1) * S * 2].bitcast(U32),
                    in_=pairs[:].bitcast(U32).indirect(offs_sb[:]),
                )
            nc.vector.tensor_copy(
                out=x_grouped[:].rearrange("p (s u e) -> p s u e", u=2, e=2),
                in_=gathered[:].rearrange("p (u s e) -> p s u e", u=2, e=2),
            )
            x_codes.append(keep.tile([P, S], U32, name="x_codes%d" % g, align_bytes=64))
            x_scales.append(keep.tile([P, S], U8, name="x_scales%d" % g, align_bytes=64))
            nc.vector.quantize_mx(out=x_codes[g][:].bitcast(FP8X4), scales=x_scales[g][:], in_=x_grouped[:])

        t_ = {}

        def w1_copy(e, g):
            t_["w1g", e, g] = keep.tile(
                [P, 4 * H], BF16, name="w1_grouped%d%d" % (e, g), tag="w1_grouped%d%d" % (e, g), align_bytes=64
            )
            grouped = t_["w1g", e, g][:].rearrange("p (t m j) -> p m j t", t=4, j=4)
            if e == E - 1 and g == G - 1:
                for half in range(2):
                    shared_copy(
                        grouped[:, half * (P // 2) : (half + 1) * (P // 2)],
                        w1_raw[e, g][half][:].rearrange("p j (m t) -> p m j t", t=4),
                        W1_SHARES_LAST,
                    )
                return
            shared_copy(grouped, (w1_raw[e, g] if e == 0 else w1_raw[e, g][:]).rearrange("p j (m t) -> p m j t", t=4), W1_SHARES[g])

        def w1_quant(e, g):
            pieces = (1, 1, 2) if (e == E - 1 and g == G - 1) else (4,)
            t_["w1c", e, g] = []
            t = 0
            for h, tiles in enumerate(pieces):
                width = tiles * P
                codes = keep.tile([P, width], U32, name="w1_codes%d%d%d" % (e, g, h), align_bytes=64)
                scales = keep.tile([P, width], U8, name="w1_scales%d%d%d" % (e, g, h), align_bytes=64)
                nc.vector.quantize_mx(
                    out=codes[:].bitcast(FP8X4),
                    scales=scales[:],
                    in_=t_["w1g", e, g][:, 4 * P * t : 4 * P * (t + tiles)],
                )
                for i in range(tiles):
                    t_["w1c", e, g].append((codes[:, i * P : (i + 1) * P], scales[:, i * P : (i + 1) * P]))
                t += tiles

        def w2_copy(e):
            t_["w2g", e] = keep.tile([P, 4 * N], BF16, name="w2_grouped%d" % e, align_bytes=64)
            shared_copy(
                t_["w2g", e][:].rearrange("p (c i j) -> p c j i", i=4, j=4),
                w2_raw[e][:].rearrange("p j (c i) -> p c j i", i=4),
                W2_SHARES,
            )

        def w2_quant(e):
            t_["w2c", e] = keep.tile([P, N], U32, name="w2_codes%d" % e, align_bytes=64)
            t_["w2s", e] = keep.tile([P, N], U8, name="w2_scales%d" % e, align_bytes=64)
            nc.vector.quantize_mx(out=t_["w2c", e][:].bitcast(FP8X4), scales=t_["w2s", e][:], in_=t_["w2g", e][:])

        def layer1(e):
            slots = slice(e * C, (e + 1) * C)
            acc1 = psum.tile([P, 4, C], F32, bufs=3)
            t_["acc1", e] = acc1
            for t in range(4):
                for g in range(G):
                    codes, scales = t_["w1c", e, g][t]
                    nc.tensor.matmul_mx(
                        out=acc1[:, t, :],
                        lhsT=codes.bitcast(FP8X4),
                        lhsT_scale=scales,
                        rhs=x_codes[g][:, slots].bitcast(FP8X4),
                        rhs_scale=x_scales[g][:, slots],
                        start=(g == 0),
                        stop=(g == G - 1),
                    )

        def silu(e):
            t_["hg", e] = raw.tile([P, C * 4], BF16, name="h_grouped%d" % e, tag="w1_raw%d0" % (e + 1), align_bytes=64)
            nc.scalar.activation(
                out=t_["hg", e][:].rearrange("p (c t) -> p c t", t=4),
                in_=t_["acc1", e][:].rearrange("p t c -> p c t"),
                func=SILU,
            )

        def h_quant(e):
            t_["hc", e] = keep.tile([P, C], U32, name="h_codes%d" % e, tag="w1_grouped%d0" % (e + 1), align_bytes=64)
            t_["hs", e] = keep.tile([P, C], U8, name="h_scales%d" % e, align_bytes=64)
            nc.vector.quantize_mx(out=t_["hc", e][:].bitcast(FP8X4), scales=t_["hs", e][:], in_=t_["hg", e][:])

        def layer2(e):
            if e == E - 1:
                banks = [psum.tile([P, C], F32, name="acc2_last%d" % b, bufs=1) for b in range(NB)]
                t_["acc2b", e] = banks
            else:
                acc2 = psum.tile([P, NB, C], F32, bufs=3)
                t_["acc2", e] = acc2
            for b in range(NB):
                cols = slice(b * P, (b + 1) * P)
                nc.tensor.matmul_mx(
                    out=banks[b][:] if e == E - 1 else acc2[:, b, :],
                    lhsT=t_["w2c", e][:, cols].bitcast(FP8X4),
                    lhsT_scale=t_["w2s", e][:, cols],
                    rhs=t_["hc", e][:].bitcast(FP8X4),
                    rhs_scale=t_["hs", e][:],
                    start=True,
                    stop=True,
                )

        def gated(e):
            t_["y", e] = keep.tile([P, NB, C], F32, name="y_sb%d" % e, tag="w1_grouped%d1" % (e + 1), align_bytes=64)
            if e == E - 1:
                for b in range(NB):
                    nc.scalar.copy(out=t_["y", e][:, b, :], in_=t_["acc2b", e][b][:])
            else:
                nc.scalar.copy(out=t_["y", e][:], in_=t_["acc2", e][:])

        def gated_block(e, b):
            if b == 0:
                t_["yb", e, b] = keep.tile([P, C], F32, name="y_sb%d%d" % (e, b), tag="w1_grouped%d1" % (e + 1), align_bytes=64)
            else:
                t_["yb", e, b] = keep.tile([P, C], F32, name="y_sb%d%d" % (e, b), tag="w2_grouped%d" % (e + 1), align_bytes=64)
            nc.scalar.copy(out=t_["yb", e, b][:], in_=t_["acc2", e][:, b, :])

        def scatter(e, b):
            nc.vector.tensor_tensor(
                out=win[b][:].indirect(offs_sb[:, e * (C // 16) : (e + 1) * (C // 16)]),
                in0=t_["yb", e, b][:] if ("yb", e, b) in t_ else t_["y", e][:, b, :],
                in1=gate_sb[e // 2][:, b, (e % 2) * C : (e % 2 + 1) * C],
                op=MULT,
            )

        for e in range(E):
            p = e - 1
            w1_copy(e, 0)
            if p >= 0:
                silu(p)
            w1_quant(e, 0)
            w1_copy(e, 1)
            if p >= 0:
                h_quant(p)
                layer2(p)
            w2_copy(e)
            w1_quant(e, 1)
            layer1(e)
            if 0 <= p < E - 2:
                gated(p)
                scatter(p, 0)
            if p == E - 2:
                gated_block(p, 0)
                scatter(p, 0)
            w2_quant(e)
            if 0 <= p < E - 2:
                scatter(p, 1)
        gated_block(E - 2, 1)
        scatter(E - 2, 1)
        silu(E - 1)
        h_quant(E - 1)
        layer2(E - 1)
        gated(E - 1)
        scatter(E - 1, 0)
        scatter(E - 1, 1)

        for b in range(NB):
            nc.sync.dma_start(out[b * P : (b + 1) * P, :], win[b][:])
